import numpy as np, ml_dtypes
CORES = [35,38,43,46]
N = 4
BF = ml_dtypes.bfloat16
B, W, CAP, RO = 1024, 8192, 64, 4
L = N * CAP
def parts(rng):
    share = rng.choice(np.array([0.1, 0.2, 0.4, 0.6]), (N, 8, 1, B))
    v = np.where(rng.random((N, 8, 16, B)) < share, -rng.integers(1, 256, (N, 8, 16, B)), rng.integers(0, 256, (N, 8, 16, B)))
    a = rng.integers(0, 256, (N, 8, 16, W)) * (rng.random((N, 8, 16, W)) < rng.choice(np.array([0.3, 0.6, 0.9]), (N, 8, 1, W))); a[..., W - 1] = 0
    u = rng.integers(0, W - 1, (N, 8, 16, B))
    u = np.where(rng.random(u.shape) < rng.choice(np.array([0.0, 0.0, 0.1, 0.1, 0.4, 0.96]), (N, 8, 1, B)), W - 1, u)
    to = np.where(rng.random((N, 8, W)) < rng.choice(np.array([0.0, 0.1, 0.25]), (N, 8, 1)), rng.integers(0, N, (N, 8, 1)), rng.integers(0, N, (N, 8, W)))
    pay = to * B + rng.integers(0, B, (N, 8, W))
    wk = np.where(rng.random((N, 8, L)) < 0.04, B, rng.integers(0, B, (N, 8, L)))
    return v, a, u, pay, wk
def pack(v, a, u, pay, wk):
    return {"vp": np.ascontiguousarray(v.reshape(N, 128, B)).astype(np.float32).astype(BF), "am": np.ascontiguousarray(a.reshape(N, 128, W)).astype(np.float32).astype(BF),
            "qu": np.ascontiguousarray(u.reshape(N, 128, B)).astype(np.int32), "pay": np.ascontiguousarray(pay).astype(np.int32), "wk": np.ascontiguousarray(wk).astype(np.int32)}
def setup_inputs(rng):
    return pack(*parts(rng))
def plant(rng, v, a, u, pay, wk, q, g, to):
    m = len(to); lanes = rng.permutation(L)[:m]; banks = rng.permutation(B)[:m]; lines = rng.permutation(W - 1)[:m]
    row = rng.integers(0, 16, m); j = rng.integers(0, 16, m)
    u[q, g][:, banks] = W - 1; u[q, g][row, banks] = lines
    v[q, g][j, banks] = -rng.integers(1, 256, m); a[q, g][j, lines] = 255
    order = np.argsort(lanes); pay[q, g][lines[order]] = to
    wk[q, g] = B; wk[q, g][lanes] = banks
def setup_inputs_room(rng):
    v, a, u, pay, wk = parts(rng)
    for q in range(N):
        for g in range(8):
            cnt = [CAP, CAP + 1, CAP - 1, 0, 1, 0, 2, CAP // 2][:N]
            if (q + g) % 4 == 3: cnt = [L] + [0] * (N - 1)
            to = np.concatenate([np.full(n, (q + 1 + g + j) % N, np.int64) for j, n in enumerate(cnt)])
            plant(rng, v, a, u, pay, wk, q, g, rng.permutation(to) * B + rng.integers(0, B, len(to)))
    return pack(v, a, u, pay, wk)
def setup_inputs_ties(rng):
    v, a, u, pay, wk = parts(rng)
    v[:, ::2] = rng.integers(-3, 3, (N, 4, 16, B)); a[:, ::2] = rng.integers(0, 4, (N, 4, 16, W))
    v[:, 1::2] = rng.integers(-3, 2, (N, 4, 16, B)) * 85; a[:, 1::2] = rng.integers(0, 4, (N, 4, 16, W)) * 85
    a = a * (rng.random((N, 8, 1, W)) < 0.6); a[..., W - 1] = 0
    u[:, :, 15] = np.where(rng.random((N, 8, B)) < 0.4, W - 1, u[:, :, 15])
    return pack(v, a, u, pay, wk)
def setup_inputs_alike(rng):
    v, a, u, pay, wk = parts(rng)
    wk[:, 0] = rng.choice(np.array([0, B - 1, 5, B // 2]), (N, L))
    u[:, 2] = rng.choice(np.array([0, W - 2, 7, W // 2, W - 1]), (N, 16, B))
    pay[:, 4] = rng.integers(0, N, (N, W)) * B + rng.choice(np.array([0, B - 1]), (N, W))
    u[:, 6] = np.repeat(u[:, 6, :1], 16, axis=1)
    wk[:, 1::2, L - 1] = wk[:, 1::2, 0]
    return pack(v, a, u, pay, wk)
def setup_inputs_dry(rng):
    v, a, u, pay, wk = parts(rng); o = rng.permutation(8)
    wk[:, o[0]] = B; a[:, o[1]] = 0; u[:, o[2]] = W - 1; v[:, o[3]] = np.abs(v[:, o[3]])
    v[:, o[4]] = -255; a[:, o[4]] = 255; a[..., W - 1] = 0
    wk[rng.integers(0, N), o[5]] = B
    h = int(o[6]); wk[:, h] = B
    for q in range(N):
        b = int(rng.integers(1, B)); n, m = [int(i) for i in rng.permutation(W - 1)[:2]]
        wk[q, h, int(rng.integers(0, L))] = b
        v[q, h, :, b] = -rng.integers(1, 256, 16); u[q, h, :, b] = n; a[q, h, :, n] = 0; pay[q, h, n] = (q + 1) % N * B
        v[q, h, :, 0] = -rng.integers(1, 256, 16); u[q, h, :, 0] = m; a[q, h, :, m] = 255; pay[q, h, m] = rng.integers(0, N) * B + rng.integers(1, B)
    return pack(v, a, u, pay, wk)
def setup_inputs_spread(rng):
    v, a, u, pay, wk = parts(rng)
    v = (np.exp2(8 * rng.random((N, 8, 1, B))) * rng.random((N, 8, 16, B))).astype(np.int64) * np.where(rng.random((N, 8, 16, B)) < 0.4, -1, 1)
    a = (np.exp2(8 * rng.random((N, 8, 1, W))) * rng.random((N, 8, 16, W))).astype(np.int64); a[..., W - 1] = 0
    u = np.where(u == W - 1, u, ((W - 1) * rng.random(u.shape) ** 2).astype(np.int64))
    pay = pay // B * B + (B * rng.random(pay.shape) ** 2).astype(np.int64)
    wk = np.where(wk == B, B, (B * rng.random(wk.shape) ** 2).astype(np.int64))
    return pack(v, a, u, pay, wk)
def check_inputs(d):
    bad = []
    for k, lo, hi in (("vp", -255, 255), ("am", 0, 255)):
        x = np.asarray(d[k]).astype(np.float32)
        if not np.all((x >= lo) & (x <= hi)): bad.append("range of " + k)
        elif not np.all(x == np.rint(x)): bad.append("whole numbers in " + k)
    if not np.all(np.asarray(d["am"]).astype(np.float32)[..., W - 1] == 0): bad.append("zeros in the last column of am")
    for k, hi in (("qu", W - 1), ("pay", N * B - 1), ("wk", B)):
        if np.min(d[k]) < 0 or np.max(d[k]) > hi: bad.append("range of " + k)
    return bad
def reference(vp, am, qu, pay, wk):
    v = vp.astype(np.float32).astype(np.int64).reshape(N, 8, 16, B); a = am.astype(np.float32).astype(np.int64).reshape(N, 8, 16, W)
    u = qu.astype(np.int64).reshape(N, 8, 16, B); payee = pay.astype(np.int64)
    w = wk.astype(np.int64); c = np.zeros((N, 8, 16, L), np.int64)
    for rnd in range(RO):
        w2 = np.full((N, 8, L), B, np.int64); c2 = np.zeros((N, 8, 16, L), np.int64)
        for q in range(N):
            for g in range(8):
                vv, aa, uu = v[q, g], a[q, g], u[q, g]
                lane = np.nonzero(w[q, g] < B)[0]
                lane = lane[np.sort(np.unique(w[q, g][lane], return_index=True)[1])]
                b = w[q, g][lane]
                x = np.maximum(vv[:, b] - c[q, g][:, lane], -255); vv[:, b] = x
                keep = np.any(x < 0, axis=0); b, x = b[keep], x[:, keep]
                n = uu[:, b]
                score = np.sum(x[:, None, :] + aa[:, n] >= 0, axis=0)
                best = 15 - np.argmax(score[::-1], axis=0)
                p = n[best, np.arange(len(b))]
                keep = p != W - 1; b, x, best, p = b[keep], x[:, keep], best[keep], p[keep]
                keep = np.sort(np.unique(p, return_index=True)[1]); b, x, best, p = b[keep], x[:, keep], best[keep], p[keep]
                t = np.minimum(aa[:, p], np.maximum(-x, 0))
                vv[:, b] = x + t; aa[:, p] = aa[:, p] - t; uu[best, b] = W - 1
                to = payee[q, g][p]
                for r in range(N):
                    k = np.nonzero(to // B == r)[0][:CAP]; s = q * CAP + np.arange(len(k))
                    w2[r, g][s] = to[k] % B; c2[r, g][:, s] = t[:, k]
        w, c = w2, c2
    return {"yv": v.reshape(N, 128, B).astype(np.float32).astype(BF), "yw": w.astype(np.float32), "yc": c.reshape(N, 128, L).astype(np.float32).astype(BF)}

from concourse.bass import DstId, RemoteDMATransfer
from concourse.mybir import AluOpType as OP, ActivationFunctionType as AF

STEPS, B, NONE = 4, 1024, 8191
VW, AW, DUMA = 1536, 8464, 8208
BIG = 65536.0
SCRATCH = {}


def _buf(dtype, n, names, parts=128):
    for b in names.split():
        SCRATCH[b] = ("sbuf", [parts, n], dtype)


_buf("bfloat16", VW, "NV")
_buf("float32", VW, "Q")
_buf("bfloat16", B, "Vin")
_buf("int32", B, "Qin")
_buf("bfloat16", AW, "A")
_buf("bfloat16", 8192, "PT")
_buf("int32", 512, "payS payH payL")
_buf("float32", 512, "payF payA")
_buf("bfloat16", 3072, "payB")
_buf("int32", 256, "wkI", 8)
_buf("float32", 256, "wkE", 8)
_buf("float16", 256, "wkH", 8)
_buf("float16", 128, "sel8", 8)
_buf("bfloat16", 128, "sel8b", 8)
_buf("bfloat16", 256, "o8", 8)
_buf("float32", 128, "imp qg BLKf")
_buf("float32", 256, "tt lane gmA SC SP SS nF np qa aS")
_buf("int32", 8, "pc pj pg pb")
_buf("float32", 32, "cf")
_buf("float32", 16, "l16 LC LC2 Wf wa pWf pa")
_buf("uint16", 16, "WL wU pL sL pU")
_buf("float32", 8, "g8")
_buf("float32", 64, "khi klo")
_buf("bfloat16", 64, "tmp")
_buf("float16", 128, "I16 NI16 ONEh BLKh")
_buf("bfloat16", 128, "Ib BLKb B512 NB512 BLK4n BLK4k DG WBm irow MONE C16 RMx HALF ZERO BIGW")
_buf("bfloat16", 8, "SB8")
_buf("bfloat16", 1024, "WT")
_buf("bfloat16", 256, "gmB gmC GM GM2 ONEb thr SD y nx mm D1 D2 PG Ap t ta OA c0")
_buf("float16", 256, "rowl KM Z")
_buf("float16", 16, "SR")
_buf("uint16", 256, "nU bR pR")
_buf("bfloat16", 4096, "eq G cmp")
for _s in range(STEPS):
    _buf("bfloat16", 1280, "WB%d WC%d" % (_s, _s))
    _buf("bfloat16", 256, "LB%d LD%d" % (_s + 1, _s + 1))
PSUM = ["k%d" % s for s in range(8)]
for _s in PSUM:
    SCRATCH[_s] = ("psum", [128, 512], "float32")
SEMAPHORES = ["sv", "ss", "st", "sg", "lb", "lc"] + ["rb%d" % s for s in range(STEPS)] + ["rc%d" % s for s in range(STEPS)] + ["d%d" % k for k in range(30)]


def split_engines(topo, cores, src):
    dst = [c for c in cores if c != src]
    off = [c for c in dst if topo.chip(c) != topo.chip(src)]
    on = [c for c in dst if topo.chip(c) == topo.chip(src)]
    out, used = {}, []
    for group in (off, on):
        if not group:
            continue
        free = [e for e in topo.engines(src, group[0]) if e not in used]
        n = 1
        while 2 * n * len(group) <= len(free):
            n *= 2
        for k, c in enumerate(group):
            out[c] = free[k * n:(k + 1) * n]
            used = used + out[c]
    return out


def rank_program(g, core, T, topo):
    q = T.rank_of(core)
    if q is None:
        return
    cores = list(T.cores)
    queue = {"v": g.vector, "s": g.scalar, "t": g.tensor, "g": g, "y": g.sync}
    semof = {"v": "sv", "s": "ss", "t": "st", "g": "sg"}
    cnt = {"sv": 0, "ss": 0, "st": 0, "sg": 0}
    know = {e: {} for e in queue}
    snap, lastw, readers, total = {}, {}, {}, {}
    ndma = [0]

    def need_wait(e, sem, val):
        if know[e].get(sem, 0) >= val:
            return
        queue[e].wait_ge(T.sem[sem], val)
        for s2, v2 in snap.get((sem, val), {}).items():
            know[e][s2] = max(know[e].get(s2, 0), v2)
        know[e][sem] = max(know[e].get(sem, 0), val)

    def waits(e, R, W, X=()):
        need = {}
        for b in R:
            if b in lastw:
                s, v = lastw[b]
                need[s] = max(need.get(s, 0), v)
        for b in list(W) + list(X):
            deps = list(readers.get(b, {}).items())
            if b in lastw:
                deps.append(lastw[b])
            for s, v in deps:
                if s != semof.get(e) or (e != "t" and b in W):
                    need[s] = max(need.get(s, 0), v)
        for s in sorted(need):
            need_wait(e, s, need[s])

    def note(sem, val, R, W, e):
        sn = dict(know[e])
        sn[sem] = val
        snap[(sem, val)] = sn
        total[sem] = val
        for b in R:
            readers.setdefault(b, {})[sem] = val
        for b in W:
            lastw[b] = (sem, val)
            readers[b] = {}

    def op(e, name, R, W, *a, **k):
        waits(e, R, W, [b for b in R if b in PSUM and b not in W])
        eng = queue[e]
        call = {"tc": lambda: eng.tensor_copy(*a), "tt": lambda: eng.tensor_tensor(*a), "ts": lambda: eng.tensor_scalar(*a),
                "scan": lambda: eng.tensor_tensor_scan(*a), "ms": lambda: eng.memset(*a), "act": lambda: eng.activation(*a, **k),
                "mm": lambda: eng.matmul(*a), "iota": lambda: eng.iota(*a, **k)}[name]
        sem = semof[e]
        cnt[sem] += 1
        call().then_inc(T.sem[sem], 1)
        note(sem, cnt[sem], R, W, e)

    def dma(e, R, W, out, in_):
        waits(e, R, W)
        sem = "d%d" % ndma[0]
        ndma[0] += 1
        queue[e].dma_start(out, in_).then_inc(T.sem[sem], 16)
        note(sem, 16, R, W, e)

    def v(name, R, W, *a):
        op("v", name, R, W, *a)

    def ts(R, W, out, in_, *a):
        v("ts", R, [W], out, in_, *a)

    def act(R, W, out, in_, func=AF.Copy, **k):
        op("s", "act", R, W, out, in_, func, **k)

    def mm(R, W, out, lhsT, rhs, start=True, stop=True):
        op("t", "mm", R, W, out, lhsT, rhs, start, stop)

    dma("y", [], ["wkI"], T.wkI[:], T.wk[:])
    dma("y", [], ["payS"], T.payS[:], T.pay[:])
    dma("y", [], ["Qin"], T.Qin[:], T.qu[:])
    dma("y", [], ["Vin"], T.Vin[:], T.vp[:])
    dma("y", [], ["Am"], T.A[:, 0:8192], T.am[:])

    def iota(buf, out, pattern, base, cm):
        op("g", "iota", [], [buf], out, pattern, base, cm, allow_small_or_imprecise_dtypes=True)
    iota("pc", T.pc[:, 0:1], [[1, 1]], 0, 1)
    iota("qg", T.qg[:], [[1, 8], [0, 16]], 0, 0)
    iota("khi", T.khi[:], [[1, 2], [0, 32]], 32 + 2 * q, 0)
    iota("klo", T.klo[:], [[0, 2], [1, 32]], 0, 0)
    iota("tt", T.tt[:], [[0, 16], [1, 16]], 0, 0)
    iota("imp", T.imp[:], [[1, 128]], 0, -1)
    iota("g8", T.g8[:], [[1, 8]], 0, 0)
    iota("lane", T.lane[:], [[1, 256]], 0, 0)
    iota("l16", T.l16[:], [[16, 16]], 0, 0)

    col = {}

    def c(name):
        return T.cf[:, col[name]:col[name] + 1]

    def colop(name, R, call, *a):
        col[name] = len(col)
        v(call, R, [name], c(name), *a)
    v("ms", [], ["ZERO"], T.ZERO[:], 0.0)
    v("ms", [], ["NVp"], T.NV[:, B:VW], 0.0)
    v("ms", [], ["Qp"], T.Q[:, B:VW], float(NONE))
    v("ms", [], ["Apd"], T.A[:, 8192:AW], 0.0)
    v("ms", [], ["c0"], T.c0[:], 0.0)
    v("ms", [], ["ONEb"], T.ONEb[:], 1.0)
    v("ms", [], ["MONE"], T.MONE[:], -1.0)
    v("ms", [], ["HALF"], T.HALF[:], 0.5)
    v("ms", [], ["C16"], T.C16[:], 16384.0)
    ts(["pc"], "pj", T.pj[:, 0:1], T.pc[:, 0:1], 15, None, OP.bitwise_and)
    ts(["pc"], "pg", T.pg[:, 0:1], T.pc[:, 0:1], 4, None, OP.arith_shift_right)
    colop("jf", ["pj"], "tc", T.pj[:, 0:1])
    colop("gf", ["pg"], "tc", T.pg[:, 0:1])
    colop("pf", ["pc"], "tc", T.pc[:, 0:1])
    colop("ja", ["jf"], "ts", c("jf"), 4.0, None, OP.is_equal)
    colop("jb", ["jf"], "ts", c("jf"), 5.0, None, OP.is_equal)
    ts(["khi", "ja"], "khi", T.khi[:], T.khi[:], c("ja"), None, OP.mult)
    ts(["klo", "jb"], "klo", T.klo[:], T.klo[:], c("jb"), None, OP.mult)
    v("tt", ["khi", "klo"], ["tmp"], T.tmp[:], T.khi[:], T.klo[:], OP.add)
    pf8 = T.cf[0:8, col["pf"]:col["pf"] + 1]
    ts(["qg", "pf"], "sel8", T.sel8[:], T.qg[0:8, :], pf8, None, OP.is_equal)
    ts(["qg", "pf"], "sel8b", T.sel8b[:], T.qg[0:8, :], pf8, None, OP.is_equal)
    colop("corr", ["jf"], "ts", c("jf"), 15.0, BIG, OP.is_lt, OP.mult)
    ts(["tt", "jf"], "gmA", T.gmA[:], T.tt[:], c("jf"), None, OP.subtract)
    ts(["gmA"], "gmB", T.gmB[:], T.gmA[:], 0.0, -4.0 * BIG, OP.is_le, OP.mult)
    ts(["gmA"], "gmC", T.gmC[:], T.gmA[:], 1.0, BIG, OP.is_equal, OP.mult)
    v("tt", ["gmB", "gmC"], ["GM"], T.GM[:], T.gmB[:], T.gmC[:], OP.add)
    for s in range(STEPS):
        for r in range(4):
            act(["tmp"], ["WB%d" % s], T["WB%d" % s][:, r * 256:r * 256 + 64], T.tmp[:])
            act(["ZERO"], ["WC%d" % s], T["WC%d" % s][:, r * 256:r * 256 + 64], T.ZERO[:, 0:64])
    ts(["wkI"], "wkE", T.wkE[:], T.wkI[:], float(B), None, OP.is_ge)
    v("tt", ["wkE", "lane"], ["wkE"], T.wkE[:], T.wkE[:], T.lane[0:8, :], OP.mult)
    v("tt", ["wkI", "wkE"], ["wkH"], T.wkH[:], T.wkI[:], T.wkE[:], OP.add)
    ts(["imp"], "Ib", T.Ib[:], T.imp[:], 0.0, None, OP.is_equal)
    ts(["qg", "gf"], "BLKb", T.BLKb[:], T.qg[:], c("gf"), None, OP.is_equal)
    colop("j4", ["jf"], "ts", c("jf"), 4.0, None, OP.is_lt)
    colop("j15", ["jf"], "ts", c("jf"), 15.0, 16384.0, OP.is_equal, OP.mult)
    v("tc", ["payS"], ["payF"], T.payF[:], T.payS[:])
    v("tc", ["Qin"], ["Qm"], T.Q[:, 0:B], T.Qin[:])
    ts(["payF", "j15"], "payF", T.payF[:, 511:512], T.payF[:, 511:512], c("j15"), None, OP.add)
    ts(["payS"], "payH", T.payH[:], T.payS[:], 5, 31, OP.arith_shift_right, OP.bitwise_and)
    v("tc", ["payH"], ["b4"], T.payB[:, 2048:2560], T.payH[:])
    ts(["payS"], "payL", T.payL[:], T.payS[:], 31, None, OP.bitwise_and)
    v("tc", ["payL"], ["b5"], T.payB[:, 2560:3072], T.payL[:])
    act(["Vin"], ["NVm"], T.NV[:, 0:B], T.Vin[:], AF.Copy, scale=-1.0)
    for r in range(4):
        act(["payF"], ["payA"], T.payA[:], T.payF[:], AF.Abs, bias=-1024.0 * r - 511.5)
        act(["payA"], ["b%d" % r], T.payB[:, 512 * r:512 * r + 512], T.payA[:], AF.Relu, bias=-512.0)
    for j in range(16):
        k = min(j, 5)
        dma("y", ["b%d" % k], ["PT%d" % j], T.PT[j::16, :], T.payB[:, 512 * k:512 * k + 512])

    def consts2():
        for k in range(4):
            ts(["pj"], "pb%d" % k, T.pb[:, k:k + 1], T.pj[:, 0:1], k, 1, OP.arith_shift_right, OP.bitwise_and)
        for k in range(4):
            colop("f%d" % k, ["pb%d" % k], "ts", T.pb[:, k:k + 1], 2.0 ** -(2 ** k) - 1.0, 1.0, OP.mult, OP.add)
        colop("f01", ["f0", "f1"], "tt", c("f0"), c("f1"), OP.mult)
        colop("f23", ["f2", "f3"], "tt", c("f2"), c("f3"), OP.mult)
        colop("pw", ["f01", "f23"], "tt", c("f01"), c("f23"), OP.mult)
        for h in range(2):
            v("scan", ["HALF", "ZERO"], ["thr"], T.thr[:, 128 * h:128 * h + 128], T.HALF[:], T.ZERO[:], 5.0 * 2.0 ** 63, OP.mult, OP.add)
        ts(["BLKb"], "BIGW", T.BIGW[:], T.BLKb[:], 2.0 ** 95, None, OP.mult)
        for k in range(8):
            ts(["BLKb", "pw"], "WT%d" % k, T.WT[:, 128 * k:128 * k + 128], T.BLKb[:], c("pw"), 2.0 ** (63 - 16 * k), OP.mult, OP.mult)
        ts(["g8", "gf"], "SB8", T.SB8[:], T.g8[:], c("gf"), None, OP.is_equal)
        ts(["tt"], "irow", T.irow[:], T.tt[:, 0:128], 1 / 16, -0.46875, OP.mult, OP.add)
        ts(["tt"], "RMx", T.RMx[:], T.tt[:, 0:128], 0.0, -1024.0, OP.is_equal, OP.mult)
        ts(["imp"], "I16", T.I16[:], T.imp[:], 0.0, None, OP.is_equal)
        ts(["imp"], "NI16", T.NI16[:], T.imp[:], 0.0, -1.0, OP.is_equal, OP.mult)
        ts(["GM"], "GM2", T.GM2[:], T.GM[:], 4.0, -8.0, OP.min, OP.max)
        colop("jc2", ["jf"], "ts", c("jf"), 1 / 16, -0.46875, OP.mult, OP.add)
        colop("icol", ["jf"], "ts", c("jf"), 256.0, -1024.0, OP.mult, OP.add)
        colop("corr2", ["jf"], "ts", c("jf"), 15.0, 4.0, OP.is_lt, OP.mult)
        colop("los", ["corr2"], "ts", c("corr2"), 1.0, None, OP.add)
        colop("ja32", ["ja"], "ts", c("ja"), 32.0, None, OP.mult)
        colop("jw", ["ja32", "jb"], "tt", c("ja32"), c("jb"), OP.add)
        ts(["BLKb"], "B512", T.B512[:], T.BLKb[:], 512.0, None, OP.mult)
        ts(["BLKb"], "NB512", T.NB512[:], T.BLKb[:], -512.0, None, OP.mult)
        v("tc", ["BLKb"], ["BLKf"], T.BLKf[:], T.BLKb[:])
        v("tc", ["BLKb"], ["BLKh"], T.BLKh[:], T.BLKb[:])
        ts(["Ib", "j4"], "DG", T.DG[:], T.Ib[:], c("j4"), 2.0 ** 95, OP.mult, OP.mult)
        ts(["qg"], "ONEh", T.ONEh[:], T.qg[:], 0.0, 1.0, OP.mult, OP.add)
        ts(["BLKb", "j4"], "BLK4n", T.BLK4n[:], T.BLKb[:], c("j4"), -1.0, OP.mult, OP.mult)
        ts(["BLKb", "j4"], "BLK4k", T.BLK4k[:], T.BLKb[:], c("j4"), 8192.0, OP.mult, OP.mult)
        ts(["BLKb", "jw"], "WBm", T.WBm[:], T.BLKb[:], c("jw"), None, OP.mult)
        ts(["lane"], "rowl", T.rowl[:], T.lane[:], 1024.0, None, OP.add)
        ts(["l16", "jf"], "LC", T.LC[:], T.l16[:], c("jf"), 1280.0, OP.add, OP.add)
        ts(["l16", "jf"], "LC2", T.LC2[:], T.l16[:], c("jf"), float(DUMA), OP.add, OP.add)

    PTs = ["PT%d" % j for j in range(16)]
    route = split_engines(topo, cores, core)
    arrive = sum(len(split_engines(topo, cores, s)[core]) for s in cores if s != core)
    nlocal = {"lb": 0, "lc": 0}

    def exchange(win, land, rsem, lsem):
        waits("g", [win], [])
        tr = []
        for r, d in enumerate(cores):
            if d == core:
                continue
            m = 0
            for e in route[d]:
                m |= 1 << e
            tr.append(RemoteDMATransfer(dst_ids=[DstId(rid=topo.addr(d)[0], pnc=topo.addr(d)[1])], dma_engine_mask=m, remote_sem=T.sem[rsem],
                                        src=T[win][:, r * 256:r * 256 + 64], dst=T[land][:, q * 64:q * 64 + 64]))
            nlocal[lsem] += len(route[d])
        g.remote_dma_fused(tr, local_sem=T.sem[lsem])
        act([win], [land + "o"], T[land][:, q * 64:q * 64 + 64], T[win][:, q * 256:q * 256 + 64])
        lastw[land] = (rsem, arrive)
        total[rsem] = arrive

    def dd_open():
        mm(["MONE", "thr"], ["k2"], T.k2[:, 0:256], T.MONE[0:1, :], T.thr[0:1, :], True, False)

    def dd_block(h, l0, l1, Rk, Rb, Wk, Wb, stop=False):
        e, at = "eq%d_%d" % (h, l0 // 128), 256 * h + l0
        ts([Rk, Wk], e, T.eq[:, at:at + l1 - l0], Rb[:, l0:l1], Wb[:, h:h + 1], None, OP.is_equal)
        k = h % 8
        for o in (0, 128):
            a, b = max(l0, o), min(l1, o + 128)
            if a < b:
                same = h // 8 == o // 128
                mm(["WT%d" % k if same else "BIGW", e], ["k2"], T.k2[:, a:b], T.WT[:, 128 * k:128 * k + 128] if same else T.BIGW[:],
                   T.eq[:, at + a - l0:at + b - l0], False, stop)

    AA, VV, QQ = ["Am", "Apd"], ["NVm", "NVp"], ["Qm", "Qp"]

    def amounts(k):
        act(AA + ["nU"], ["g%d" % k], T.G[:, 1024 * k:1024 * k + 1024], T.A[:].indirect(T.nU[:, 64 * k:64 * k + 64]))

    def compare(l0, l1):
        h, n = l0 // 128, l1 - l0
        kk, m0 = "k%d" % (3 + h), l0 % 128
        mm(["ONEb", "irow"], [kk], T[kk][m0:m0 + n, 0:128], T.ONEb[0:1, 0:n], T.irow[0:1, :], True, False)
        gk = ["g%d" % k for k in range(l0 // 64, l1 // 64)]
        for i in range(16):
            at, ok = 256 * i + l0, "c%d_%d" % (i, l0)
            v("tt", gk + ["k1"], [ok], T.cmp[:, at:at + n], T.G[:, 16 * l0 + i:16 * l1:16], T.k1[:, l0:l1], OP.is_ge)
            mm([ok, "SB8"], [kk], T[kk][m0:m0 + n, i:128:16], T.cmp[:, at:at + n], T.SB8[:], False, i == 15)

    def best(h):
        kk, o = "k%d" % (3 + h), 128 * h
        v("scan", ["RMx", kk], ["KM%d" % h], T.KM[:, o:o + 128], T.RMx[:], T[kk][:, 0:128], 0.0, OP.add, OP.max)
        ts(["KM%d" % h], "SR%d" % h, T.SR[:, 8 * h:8 * h + 8], T.KM[:, o + 15:o + 128:16], 12582912.0, 12582912.0, OP.add, OP.subtract)
        mm(["KM%d" % h, "I16"], ["k7"], T.k7[0:8, o:o + 128], T.KM[:, o + 15:o + 128:16], T.I16[:], True, False)
        mm(["SR%d" % h, "NI16"], ["k7"], T.k7[0:8, o:o + 128], T.SR[:, 8 * h:8 * h + 8], T.NI16[:], False, True)

    def rows(h, e):
        o = 128 * h
        if e == "s":
            act(["k7"], ["o8%d" % h], T.o8[:, o:o + 128], T.k7[0:8, o:o + 128])
        else:
            v("tc", ["k7"], ["o8%d" % h], T.o8[:, o:o + 128], T.k7[0:8, o:o + 128])
        mm(["sel8b", "o8%d" % h], ["k6"], T.k6[:, o:o + 128], T.sel8b[:], T.o8[:, o:o + 128])

    def pick(h):
        o = 128 * h
        ts(["k6", "jc2"], "k6", T.k6[:, 256 + o:384 + o], T.k6[:, o:o + 128], c("jc2"), None, OP.is_equal)
        v("tt", ["k6", "nF"], ["np%d" % h], T.np[:, o:o + 128], T.k6[:, 256 + o:384 + o], T.nF[:, o:o + 128], OP.mult)
        out = T.k5[:, o:o + 128]
        mm(["ONEb", "C16"], ["k5"], out, T.ONEb[0:1, 0:128], T.C16[0:1, :], True, False)
        mm(["B512", "D1"], ["k5"], out, T.B512[:], T.D1[:, o:o + 128], False, False)
        mm(["NB512", "D2"], ["k5"], out, T.NB512[:], T.D2[:, o:o + 128], False, False)
        mm(["BLKf", "np%d" % h], ["k5"], out, T.BLKf[:], T.np[:, o:o + 128], False, True)

    def lines(h):
        o, w = 128 * h, slice(8 * h, 8 * h + 8)
        v("scan", ["GM", "k5"], ["SP%d" % h], T.SP[:, o:o + 128], T.GM[:, 0:128], T.k5[:, o:o + 128], 0.0, OP.add, OP.max)
        sp = T.SP[:, o + 15:o + 128:16]
        ts(["SP%d" % h, "corr"], "pL%d" % h, T.pL[:, w], sp, c("corr"), 8191.0, OP.subtract, OP.min)
        act(PTs + ["pL%d" % h], ["PG%d" % h], T.PG[:, o:o + 128], T.PT[:].indirect(T.pL[:, w]))
        act(AA + ["pL%d" % h], ["Ap%d" % h], T.Ap[:, o:o + 128], T.A[:].indirect(T.pL[:, w]))
        ts(["SP%d" % h, "corr"], "pWf%d" % h, T.pWf[:, w], sp, c("corr"), 8191.0, OP.subtract, OP.min)
        v("tc", ["k5"], ["pR%d" % h], T.pR[:, o:o + 128], T.k5[:, o:o + 128])

    def write_banks():
        v("tt", ["nx", "ta", "wU"], VV, T.NV[:].indirect(T.wU[:]), T.nx[:], T.ta[:], OP.add)

    for s in range(STEPS):
        last = s == STEPS - 1
        if s == 0:
            mm(["sel8", "wkH"], ["k0"], T.k0[:, 0:256], T.sel8[:], T.wkH[:])
            carry, ck = T.c0, ["c0"]
        else:
            mm(["WBm", "LB%d" % s, "LB%do" % s], ["k0"], T.k0[:, 0:256], T.WBm[:], T["LB%d" % s][:])
            carry, ck = T["LD%d" % s], ["LD%d" % s, "LD%do" % s]
        v("scan", ["GM", "k0"], ["SC"], T.SC[:], T.GM[:], T.k0[:, 0:256], 0.0, OP.add, OP.max)
        ts(["SC", "corr"], "WL", T.WL[:], T.SC[:, 15::16], c("corr"), None, OP.subtract)
        v("tc", QQ + ["WL"], ["nU"], T.nU[:], T.Q[:].indirect(T.WL[:]))
        if s:
            write_banks()
        v("tt", VV + ["WL"] + ck, ["y"], T.y[:], T.NV[:].indirect(T.WL[:]), carry[:], OP.add)
        ts(["y"], "nx", T.nx[:], T.y[:], 255.0, None, OP.min)
        mm(["Ib", "nx"], ["k1"], T.k1[:, 0:256], T.Ib[:], T.nx[:])
        if s == 0:
            consts2()
        v("tc", ["k0"], ["bR"], T.bR[:], T.k0[:, 0:256])
        ts(["SC", "corr"], "Wf", T.Wf[:], T.SC[:, 15::16], c("corr"), None, OP.subtract)
        amounts(0)
        act(["nx"], ["mm"], T.mm[:], T.nx[:], AF.Relu)
        mm(["BLKb", "mm"], ["k5"], T.k5[:, 256:512], T.BLKb[:], T.mm[:])
        dd_open()
        for h in range(16):
            dd_block(h, 16 * h, 256, "bR", T.bR, "Wf", T.Wf, h == 15)
        v("tc", ["nU"], ["nF"], T.nF[:], T.nU[:])
        amounts(1)
        act(["k5"], ["D2"], T.D2[:], T.k5[:, 256:512], AF.Sign, bias=-0.5)
        amounts(2)
        act(["k2"], ["D1"], T.D1[:], T.k2[:, 0:256], AF.Sign)
        amounts(3)
        compare(0, 128)
        best(0)
        compare(128, 192)
        rows(0, "v")
        v("scan", ["GM2", "D1"], ["SD"], T.SD[:], T.GM2[:], T.D1[:], 0.0, OP.add, OP.max)
        pick(0)
        ts(["SD", "los"], "wa", T.wa[:], T.SD[:, 15::16], c("los"), None, OP.is_equal)
        v("tt", ["wa", "LC"], ["wa"], T.wa[:], T.wa[:], T.LC[:], OP.mult)
        v("tt", ["wa", "Wf"], ["wa"], T.wa[:], T.wa[:], T.Wf[:], OP.max)
        v("tc", ["wa"], ["wU"], T.wU[:], T.wa[:])
        compare(192, 256)
        best(1)
        rows(1, "s")
        lines(0)
        mm(["Ib", "mm"], ["k3"], T.k3[:, 256:512], T.Ib[:], T.mm[:])
        dd_open()
        pick(1)
        for h in range(8):
            dd_block(h, 16 * h, 128, "pR0", T.pR, "pWf0", T.pWf)
        lines(1)
        mm(["DG", "PG0", "PG1"], ["k2"], T.k2[:, 0:256], T.DG[:], T.PG[:], False, False)
        for h in range(8):
            dd_block(h, 128, 256, "pR1", T.pR, "pWf0", T.pWf)
        for h in range(8, 16):
            dd_block(h, 16 * h, 256, "pR1", T.pR, "pWf1", T.pWf, h == 15)
        v("tt", ["Ap0", "Ap1", "k3"], ["t"], T.t[:], T.Ap[:], T.k3[:, 256:512], OP.min)
        ts(["k2", "j4"], "OA", T.OA[:], T.k2[:, 0:256], 0.0, c("j4"), OP.is_lt, OP.mult)
        mm(["BLK4n", "OA"], ["k1"], T.k1[:, 0:256], T.BLK4n[:], T.OA[:])
        if not last:
            mm(["BLK4k", "OA"], ["k4"], T.k4[:, 256:512], T.BLK4k[:], T.OA[:])
            act(["k4"], ["aS"], T.aS[:], T.k4[:, 256:512])
        mm(["ONEh", "rowl"], ["k0"], T.k0[:, 256:512], T.ONEh[0:1, :], T.rowl[0:1, :], True, False)
        v("scan", ["OA", "ONEb", "icol"], ["k7"], T.k7[:, 0:256], T.OA[:], T.ONEb[:], c("icol"), OP.add, OP.subtract)
        v("tt", ["k7", "OA"], ["Z"], T.Z[:], T.k7[:, 0:256], T.OA[:], OP.mult)
        mm(["BLKh", "Z"], ["k0"], T.k0[:, 256:512], T.BLKh[:], T.Z[:], False, True)
        v("tt", ["k1", "t"], ["ta"], T.ta[:], T.k1[:, 0:256], T.t[:], OP.mult)
        v("scan", ["GM", "k0"], ["SS"], T.SS[:], T.GM[:], T.k0[:, 256:512], 0.0, OP.add, OP.max)
        ts(["SS", "corr"], "sL", T.sL[:], T.SS[:, 15::16], c("corr"), None, OP.subtract)
        wb, wc, lb, lc = "WB%d" % s, "WC%d" % s, "LB%d" % (s + 1), "LD%d" % (s + 1)
        v("tc", ["PG0", "PG1", "sL"], [wb], T[wb][:].indirect(T.sL[:]), T.PG[:])
        exchange(wb, lb, "rb%d" % s, "lb")
        v("tc", ["t", "sL"], [wc], T[wc][:].indirect(T.sL[:]), T.t[:])
        exchange(wc, lc, "rc%d" % s, "lc")
        if last:
            write_banks()
        else:
            ts(["SS", "corr"], "pa", T.pa[:], T.SS[:, 15::16], c("corr"), 1024.0, OP.subtract, OP.is_ge)
            v("tt", ["pa", "LC2"], ["pa"], T.pa[:], T.pa[:], T.LC2[:], OP.mult)
            v("tt", ["pa", "pWf0", "pWf1"], ["pa"], T.pa[:], T.pa[:], T.pWf[:], OP.max)
            v("tc", ["pa"], ["pU"], T.pU[:], T.pa[:])
            v("tt", ["Ap0", "Ap1", "ta", "pU"], AA, T.A[:].indirect(T.pU[:]), T.Ap[:], T.ta[:], OP.add)
            v("tt", ["k6", "aS"], ["qa"], T.qa[:], T.k6[:, 256:512], T.aS[:], OP.mult)
            v("tt", ["qa", "nF", "wU"], QQ, T.Q[:].indirect(T.wU[:]), T.qa[:], T.nF[:], OP.max)
    ts(VV, "Vin", T.Vin[:], T.NV[:, 0:B], -1.0, None, OP.mult)
    dma("y", ["Vin"], ["yv"], T.yv[:], T.Vin[:])
    dma("y", ["LD4", "LD4o"], ["yc"], T.yc[:], T.LD4[:])
    mm(["WBm", "LB4", "LB4o"], ["k0"], T.k0[:, 0:256], T.WBm[:], T.LB4[:])
    ts(["k0"], "SC", T.SC[:], T.k0[:, 0:256], float(B), None, OP.min)
    dma("s", ["SC"], ["yw"], T.yw[:], T.SC[0:128:16, :])
    total["lb"], total["lc"] = nlocal["lb"], nlocal["lc"]
    for sem in sorted(total):
        need_wait("g", sem, total[sem])
